import numpy as np, ml_dtypes
CORES = [51,54,179,182]
N = 4
BF = ml_dtypes.bfloat16
def gentries(a):
    return np.ascontiguousarray(a.reshape(8, 16, -1).transpose(0, 2, 1)).reshape(8, -1)
def gtable(e):
    e = np.asarray(e); return np.ascontiguousarray(e.reshape(8, -1, 16).transpose(0, 2, 1)).reshape(128, -1).astype(np.int32)
W, C, RO = 2048, 256, 4
LA, LB, LE, WD = 832, 1024, 1040, 32
def parts(rng):
    x = rng.integers(0, 256, (N, 8, 16, W)); a = rng.integers(0, W, (N, 8, C, 16)); p = rng.integers(0, W, (N, 8, C, 16))
    pool = rng.integers(0, W, (N, 8, 32)); hot = np.take_along_axis(pool, rng.integers(0, 32, (N, 8, C * 16)), 2).reshape(N, 8, C, 16)
    return x, a, np.where(rng.random((N, 8, C, 16)) < 0.3, hot, p)
def pack(x, a, p):
    return {"x0": np.ascontiguousarray(x.reshape(N, 128, W)).astype(np.float32).astype(BF), "ka": np.stack([gtable(v.reshape(8, -1)) for v in a]), "ph": np.stack([gtable(v.reshape(8, -1)) for v in p])}
def alike(rng, a, p, share):
    m = (rng.random((N, 8, C, 1)) < share) & (np.arange(16) == rng.integers(0, 16, (N, 8, C, 1)))
    return np.where(m, a, p)
def setup_inputs(rng):
    x, a, p = parts(rng)
    return pack(x, a, alike(rng, a, p, 0.08))
def setup_inputs_spread(rng):
    x, a, p = parts(rng)
    v = np.minimum((np.exp2(8 * rng.random((N, 8, 1, W))) * rng.random(x.shape)).astype(np.int64), 255)
    x = np.where(rng.random(x.shape) < 0.5, v, 255 - v)
    a = np.minimum((W * rng.random(a.shape) ** 2).astype(np.int64), W - 1); u = np.minimum((W * rng.random(a.shape) ** 3).astype(np.int64), W - 1)
    return pack(x, a, np.where(rng.random(a.shape) < 0.5, u, p))
def setup_inputs_ends(rng):
    x, a, p = parts(rng); x = 255 * rng.integers(0, 2, x.shape)
    h = rng.choice(np.array([3, 4, 4, 5, 16]), (N, 8)); h[N - 1, 7] = 16; h[0, 7] = 4; h[0, 0] = 4; h[0, 1] = 3; h[N - 1, 6] = 4
    for r in range(N):
        for g in range(8):
            w = x[r, g]; w[:, W - 1] = w[:, 0]; o = rng.permutation(16)[:h[r, g]]
            if h[r, g] == 16: w[:, 0] = 0
            w[o, W - 1] = 255 - w[o, 0]
    kind = rng.choice(np.array([0, 1, 2]), (N, 8, C, 1), p=[0.4, 0.34, 0.26]); kind[:, :, [0, 1, 3, C - 2, C - 1]] = 0
    e = rng.integers(0, 2, (N, 8, C, 1))
    a = np.where(kind == 0, e * (W - 1), np.where(kind == 1, (W - 1) * rng.integers(0, 2, a.shape), a))
    p = np.where(kind == 0, (1 - e) * (W - 1), np.where(kind == 1, (W - 1) * rng.integers(0, 2, a.shape), p))
    return pack(x, a, p)
def setup_inputs_corners(rng):
    x = np.zeros((N, 8, 16, W), np.int64); a = np.zeros((N, 8, C, 16), np.int64); p = np.zeros((N, 8, C, 16), np.int64)
    far = np.array([LA - 1, LA, LA + 1, LB - 1, LB, LB + 3, LB + 4, LB + 59, LB + 60]); h = W // 2; M = 36; lane = np.arange(16)
    signs = np.stack([np.ones(16, np.int64), -np.ones(16, np.int64), 1 - 2 * (lane & 1)])
    for g in range(8):
        q = rng.permutation(W); low = q[1:h]; high = q[h + M:]; mids = q[h:h + M]
        m0 = rng.choice(np.array([-1, 0, 15, 15, 6]), C); o = lane[None, :] == m0[:, None]; o = o ^ (rng.random((C, 1)) < 0.5)
        k = rng.integers(0, 16, C); k = np.where(k == m0, (k + 1) & 15, k); swap = rng.random(C) < 0.5
        for r in range(N):
            w = x[r, g]; w[:, low] = rng.integers(0, 31, (16, len(low))); w[:, high] = rng.integers(215, 256, (16, len(high)))
            b = rng.integers(100, 151, 16); w[:, q[0]] = b; T = rng.permutation(np.resize(far, M))
            am = T[None, :] // 16 + (lane[:, None] < T[None, :] % 16); w[:, mids] = b[:, None] + am * signs[rng.integers(0, 3, M)].T
            lo1 = low[rng.integers(0, len(low), (C, 16))]; lo2 = low[rng.integers(0, len(low), (C, 16))]; hi1 = high[rng.integers(0, len(high), (C, 16))]; hi2 = high[rng.integers(0, len(high), (C, 16))]
            u = np.where(o, hi1, lo1); v = np.where(o, lo2, hi2)
            n = (0, 16, 15, C, 1, 17, 14, 31)[(g + 3 * r) % 8]; oc = rng.permutation(C); die = oc[:n]; rest = oc[n:]
            v[die, k[die]] = np.where(o[die, k[die]], hi2[die, k[die]], lo2[die, k[die]])
            edge = die[1::2]; under = mids[T == LA - 1]; md = under[rng.integers(0, len(under), len(edge))]
            u[edge, k[edge]] = np.where(swap[edge], md, q[0]); v[edge, k[edge]] = np.where(swap[edge], q[0], md)
            over = mids[T >= LA]; md = over[rng.integers(0, len(over), len(rest))]
            u[rest, k[rest]] = np.where(swap[rest], md, q[0]); v[rest, k[rest]] = np.where(swap[rest], q[0], md)
            assert int(np.sum(np.min(np.add.reduce(np.abs(w[:, u] - w[:, v]), axis=0), axis=1) < LA)) == n
            a[r, g] = u; p[r, g] = v
    return pack(x, a, p)
def setup_inputs_full(rng):
    x, a, p = parts(rng); lane = np.arange(16); h = W // 2; u = W // 4; z = int(rng.integers(0, N)); dead = int(rng.integers(0, 8))
    for g in range(8):
        if g == dead: continue
        for r in range(N):
            w = x[r, g]; q = rng.permutation(W); right = q[:h]; left = q[h:h + u]; out = q[h + u:]; b = rng.integers(100, 151, (16, 1))
            w[:, right] = b + rng.integers(0, 4, (16, h))
            far = np.where(rng.random((16, u)) < 0.5, 78 + rng.integers(0, 3, (16, u)), -75 - rng.integers(0, 3, (16, u)))
            near = np.argsort(rng.random((16, u)), axis=0) < 4
            w[:, left] = b + np.where(near, rng.integers(-8, 12, (16, u)), far)
            w[:, out] = b + rng.integers(90, 100, (16, len(out))) * (1 - 2 * rng.integers(0, 2, (16, len(out))))
            i = (rng.permutation(h)[:C], np.full(C, int(rng.integers(0, h))), rng.integers(0, 6, C))[(g + r) % 3]
            here = lane[None, :] == rng.integers(0, 16, (C, 1))
            a[r, g] = np.where(here, left[rng.integers(0, u, (C, 16))], right[rng.integers(0, h, (C, 16))])
            p[r, g] = np.where(here, right[i][:, None], out[rng.integers(0, len(out), (C, 16))])
    q = rng.permutation(np.arange(1, W)); s1 = q[:h]; s2 = q[h:h + u]; s0 = np.append(q[h + u:], 0)
    a[:, dead] = 0; p[:, dead] = s0[rng.integers(0, len(s0), (N, C, 16))]
    far = np.array([LB - 1, LB, LB + 1, LB + 3, LB + 4, LB + 31, LB + 59, LB + 60]); T = far[np.arange(h) % 8]
    cl = np.minimum(rng.integers(0, 8, (C, 1)) + rng.integers(0, 3, (C, 16)), 7)
    a[(z - 2) % N, dead] = s1[cl + 8 * rng.integers(0, h // 8, (C, 16))]; p[(z + 2) % N, dead] = s2[rng.integers(0, u, (C, 16))]
    x[:, dead] = rng.integers(215, 256, (N, 16, W))
    for r in range(N):
        w = x[r, dead]; w[:, s1] = rng.integers(0, 31, (16, h))
        if r == z:
            b = rng.integers(100, 151, (16, 1)); w[:] = b + rng.integers(0, 4, (16, W)); w[:, s2] = b
            w[:, s1] = b + (T[None, :] // 16 + (lane[:, None] < T[None, :] % 16)) * (1 - 2 * rng.integers(0, 2, (16, h)))
    return pack(x, a, p)
def setup_inputs_ties(rng):
    x, a, p = parts(rng); x = rng.integers(0, 176, x.shape)
    pool = rng.integers(0, W, (N, 8, 8)); pool[..., 0] = 0; pool[..., 7] = W - 1
    hot = np.take_along_axis(pool, rng.integers(0, 8, (N, 8, C * 16)), 2).reshape(N, 8, C, 16); p[:, 1::2] = hot[:, 1::2]
    src = np.arange(16) % rng.choice(np.array([1, 1, 1, 2, 4, 16]), (N, 8, C, 1))
    return pack(x, np.take_along_axis(a, src, 3), np.take_along_axis(p, src, 3))
def check_inputs(d):
    bad = []
    for k, lo, hi in (("x0", 0, 255), ("ka", 0, W - 1), ("ph", 0, W - 1)):
        v = np.asarray(d[k]).astype(np.float64)
        if not (np.min(v) >= lo and np.max(v) <= hi): bad.append("range of " + k)
    v = np.asarray(d["x0"]).astype(np.float64)
    if np.any(v != np.floor(v)): bad.append("whole numbers of x0")
    return bad
def reference(x0, ka, ph):
    X = x0.astype(np.float32).astype(np.int32).reshape(N, 8, 16, W)
    K = np.stack([gentries(v) for v in ka]).astype(np.int64).reshape(N, 8, C, 16)
    P = np.stack([gentries(v) for v in ph]).astype(np.int64).reshape(N, 8, C, 16)
    A = np.zeros((N, 8, 1), np.int64); place = np.arange(16)
    for t in range(RO):
        if t > 0: K = np.roll(K, 1, axis=0); P = np.roll(P, -1, axis=0)
        for r in range(N):
            x, a, p = X[r], K[r].copy(), P[r].copy()
            s = np.take_along_axis(x, a.reshape(8, 1, C * 16), 2).reshape(8, 16, C, 16); y = np.take_along_axis(x, p.reshape(8, 1, C * 16), 2).reshape(8, 16, C, 16)
            D = np.add.reduce(np.abs(s - y), axis=1)
            k = np.argmin(D, axis=2)
            d = np.take_along_axis(D, k[:, :, None], 2)[:, :, 0]
            sk = np.take_along_axis(s, k[:, None, :, None], 3)[..., 0]; yk = np.take_along_axis(y, k[:, None, :, None], 3)[..., 0]
            kill = d < LA; prime = ~kill & (d < LB + 4 * (A[r] & 15))
            step = np.where(np.add.reduce(sk, axis=1) > np.add.reduce(yk, axis=1), 1, -1) * (1 + (d & 3))
            n = np.take_along_axis(p, ((k + step) & 15)[:, :, None], 2)[:, :, 0]
            xn = np.take_along_axis(x, n[:, None, :], 2)
            near = np.add.reduce(np.abs(s - xn[..., None]), axis=1) < LE
            m = np.where(np.any(near, axis=2), np.argmax(near, axis=2), -1)
            fresh = np.take_along_axis(a, np.clip(m[:, :, None] + place, 0, 15), 2); fresh[:, :, 0] = n
            v = np.take_along_axis(p, k[:, :, None], 2)[:, :, 0]; new = np.where(np.abs(sk - yk) <= WD, (yk + 128) & 255, yk)
            for g in range(8):
                c = np.nonzero(prime[g])[0]; w = c[np.unique(v[g, c], return_index=True)[1]]
                x[g][:, v[g, w]] = new[g][:, w]
            P[r] = np.where(kill[:, :, None], (((a * p) >> 5) + p) & (W - 1), p)
            K[r] = np.where(prime[:, :, None], fresh, a)
            A[r] = A[r] + np.add.reduce(kill.astype(np.int64), axis=1)[:, None]
    return {"yk": np.stack([gtable(v.reshape(8, -1)) for v in K]).astype(np.float32), "yp": np.stack([gtable(v.reshape(8, -1)) for v in P]).astype(np.float32), "yx": X.reshape(N, 128, W).astype(np.float32).astype(BF)}

@@ -1,0 +1,468 @@
+from concourse.mybir import AluOpType as Op, ActivationFunctionType as AF, AxisListType as AX
+
+RO = 4
+F, B, H, I, U = "float32", "bfloat16", "float16", "int32", "uint16"
+SCRATCH = {}
+for _n, _w, _d in (
+        ("xt0", 2304, B), ("xt1", 2304, B), ("nk", 256, I), ("np_", 256, I), ("yg", 4096, B), ("sg", 4096, B), ("eg", 4096, B),
+        ("kp", 256, F), ("p32", 256, F), ("sn", 256, F), ("code", 256, F), ("mi", 256, I),
+        ("v8", 16, I), ("l8", 16, U), ("kf", 16, B), ("lt", 16, F), ("fl", 16, F), ("fl16", 16, U),
+        ("nsel", 256, H), ("ksel", 256, H), ("nb", 256, U), ("ns", 256, F), ("pks", 256, F),
+        ("pa", 256, F), ("pt", 256, I), ("pn", 256, I), ("yp32", 256, F),
+        ("npx", 16, F), ("o1", 16, F), ("o2", 16, F), ("o16", 16, U), ("nfix", 256, F), ("wt", 8192, F), ("fr", 256, F),
+        ("yk32", 256, F), ("ew", 256, F), ("ms", 256, F), ("zf", 256, F),
+        ("rr", 256, H), ("ol", 16, F), ("eq", 4096, B), ("cs", 256, B), ("v1", 16, F), ("v2", 16, F), ("w16", 16, U),
+        ("kk", 16, I), ("ok", 16, I), ("ok16", 16, U), ("yk_", 256, B), ("dk", 256, B), ("adk", 256, B), ("sgn", 256, B),
+        ("c1", 256, B), ("tt", 256, B), ("ca", 1, F), ("aa", 1, I), ("ab", 1, I), ("thr", 1, F),
+        ("pi", 2, I), ("li", 2, I), ("lf", 2, F), ("pf", 2, F), ("pl", 2, F), ("i2", 2048, I),
+        ("dg_", 2048, B), ("ones", 128, B), ("gm", 128, B), ("tri", 128, B), ("idn", 128, B),
+        ("z1", 143, B), ("z64", 143, B), ("cj", 256, B), ("rst", 256, F), ("rs2", 256, F), ("zero", 256, B),
+        ("q16", 16, F), ("cf", 16, F), ("c16", 16, I), ("cd", 16, F), ("cw", 16, F),
+        ("lk", 256, I), ("lz", 256, I), ("ls", 256, I), ("l3", 256, I), ("l4", 256, I), ("l5", 256, I),
+        ("lutf", 256, B), ("lutk", 256, B), ("lutm", 16, F), ("luto", 16, F), ("lutp", 16, F)):
+    SCRATCH[_n] = ("sbuf", [128, _w], _d)
+for _n in ("d3", "a3", "ae"):
+    SCRATCH[_n] = ("sbuf", [128, 16, 256], B)
+SCRATCH["kd"] = ("dram", [8, 32, 256], F)
+for _t in range(RO):
+    for _h in range(2):
+        SCRATCH["k16_%d_%d" % (_t, _h)] = ("sbuf", [128, 128], U)
+        SCRATCH["ks_%d_%d" % (_t, _h)] = ("sbuf", [128, 128], U)
+    SCRATCH["p16_%d" % _t] = ("sbuf", [128, 256], U)
+    SCRATCH["ps_%d" % _t] = ("sbuf", [128, 256], U)
+PSUM = ("bT", "bT2", "bD", "bD2", "bN", "bM", "bC")
+for _n in PSUM:
+    SCRATCH[_n] = ("psum", [128, 512], F)
+SEMAPHORES = (["v", "s", "p", "g", "lx", "lp", "lk", "oy", "ok", "op", "sent", "kz", "kd", "wd"]
+              + ["ka%d_%d" % (t, h) for t in range(1, RO) for h in range(2)] + ["pa%d" % t for t in range(1, RO)]
+              + ["xc%d" % t for t in range(RO)])
+
+
+def rank_program(g, core, T, topo):
+    rank = T.rank_of(core)
+    if rank is None:
+        return
+    n_ranks = len(T.cores)
+    Q = {"v": g.vector, "s": g.scalar, "p": g.tensor, "g": g, "y": g.sync}
+    cnt = {"v": 0, "s": 0, "p": 0, "g": 0}
+    seen = {q: {} for q in Q}
+    snap, hist = {}, {}
+
+    def a(name, lo=0, hi=None, step=None):
+        hi = SCRATCH[name][1][1] if hi is None else hi
+        return (T[name][:, lo:hi] if step is None else T[name][:, lo:hi:step], name, lo, hi)
+
+    def a3(name, q0, q1, c0=None, c1=None):
+        return (T[name][:, q0:q1, :] if c0 is None else T[name][:, q0:q1, c0:c1], name, 256 * q0, 256 * q1)
+
+    def row(name, q):
+        return (T[name][:, q], name, 256 * q, 256 * q + 256)
+
+    def ind(win, off):
+        return (win[0].indirect(off[0]), win, off)
+
+    def need(q, outs, ins):
+        want = {}
+        for kind, lst in (("w", outs), ("r", ins)):
+            for _, name, lo, hi in lst:
+                bank = name in PSUM
+                for k2, l2, h2, q2, sem, val in hist.get(name, ()):
+                    if q2 == q and q != "dma" and (k2 == "r" or q == "p" and kind == "w"):
+                        continue
+                    if not (bank and q2 != q) and (k2 == kind == "r" or h2 <= lo or l2 >= hi):
+                        continue
+                    want[sem] = max(want.get(sem, 0), val)
+        return want
+
+    def waits(q, want):
+        for sem, val in sorted(want.items()):
+            if seen[q].get(sem, 0) < val:
+                Q[q].wait_ge(T.sem[sem], val)
+                seen[q][sem] = val
+                for s2, v2 in snap.get((sem, val), {}).items():
+                    seen[q][s2] = max(seen[q].get(s2, 0), v2)
+
+    def note(q, sem, val, outs, ins, known):
+        snap[(sem, val)] = dict(known)
+        for kind, lst in (("w", outs), ("r", ins)):
+            for _, name, lo, hi in lst:
+                h = hist.setdefault(name, [])
+                if kind == "w":
+                    h[:] = [e for e in h if not (e[1] >= lo and e[2] <= hi)]
+                h.append((kind, lo, hi, q, sem, val))
+
+    def flat(lst):
+        r = []
+        for x in lst:
+            r += [x] if isinstance(x[1], str) else [x[1], x[2]]
+        return r
+
+    def do(q, fn, outs, ins):
+        o, i = flat(outs), flat(ins)
+        waits(q, need(q, o, i))
+        cnt[q] += 1
+        fn().then_inc(T.sem[q], 1)
+        note(q, q, cnt[q], o, i, seen[q])
+
+    def dma(q, sem, out, in_, outs, ins):
+        waits(q, need("dma", outs, ins))
+        Q[q].dma_start(out, in_).then_inc(T.sem[sem], 16)
+        note("dma", sem, 16, outs, ins, seen[q])
+
+    V, S, P = g.vector, g.scalar, g.tensor
+
+    def copy(out, in_):
+        do("v", lambda: V.tensor_copy(out[0], in_[0]), [out], [in_])
+
+    def tt(out, x, y, op):
+        if isinstance(out[1], tuple):
+            do("v", lambda: V.tensor_tensor(out[0], x[0], y[0], op), [out[1]], [x, y, out[2]])
+        else:
+            do("v", lambda: V.tensor_tensor(out[0], x[0], y[0], op), [out], [x, y])
+
+    def ts(out, x, s1, op0, s2=None, op1=None):
+        ins = [x] + [s for s in (s1, s2) if isinstance(s, tuple)]
+        c = [s[0] if isinstance(s, tuple) else s for s in (s1, s2)]
+        if op1 is None:
+            do("v", lambda: V.tensor_scalar(out[0], x[0], c[0], None, op0), [out], ins)
+        else:
+            do("v", lambda: V.tensor_scalar(out[0], x[0], c[0], c[1], op0, op1), [out], ins)
+
+    def scan(out, d0, d1, op0, op1):
+        do("v", lambda: V.tensor_tensor_scan(out[0], d0[0], d1[0], 1000000.0, op0, op1), [out], [d0, d1])
+
+    def fill(out, val):
+        do("v", lambda: V.memset(out[0], val), [out], [])
+
+    def act(out, in_, func, **kw):
+        do("s", lambda: S.activation(out[0], in_[0], func, **kw), [out], [in_])
+
+    def mm(out, l, r, start, stop):
+        do("p", lambda: P.matmul(out[0], l[0], r[0], start, stop), [out], [l, r])
+
+    def iota(out, pattern, base, cm, **kw):
+        do("g", lambda: g.iota(out[0], pattern, base, cm, **kw), [out], [])
+
+    def asel(out, in_, pattern, cop, base, cm):
+        do("g", lambda: g.affine_select(out[0], in_[0], pattern, cop, 0.0, base, cm), [out], [in_])
+
+    dma("y", "lp", T.np_[:], T.ph[:], [a("np_")], [])
+    dma("s", "lk", T.nk[:], T.ka[:], [a("nk")], [])
+    dma("y", "lx", T.xt0[:, 0:2048], T.x0[:], [a("xt0", 0, 2048)], [])
+
+    small = dict(allow_small_or_imprecise_dtypes=True)
+    iota(a("pi"), [[0, 2]], 0, 1)
+    fill(a("ones"), 1.0)
+    asel(a("gm"), a("ones"), [[-16, 8], [0, 16]], Op.is_ge, 0, 1)
+    asel(a("gm"), a("gm"), [[16, 8], [0, 16]], Op.is_ge, 15, -1)
+    asel(a("idn"), a("ones"), [[1, 128]], Op.is_equal, 0, -1)
+    iota(a("cj"), [[0, 16], [4, 16]], 1, 0, **small)
+    iota(a("lk"), [[0, 4], [1, 16], [0, 4]], 0, 0)
+    iota(a("lz"), [[1, 4], [0, 64]], 1, 0)
+    iota(a("ls"), [[0, 64], [2, 2], [0, 2]], -1, 0)
+    iota(a("q16"), [[16, 16]], 0, 0, **small)
+    asel(a("tri"), a("gm"), [[1, 128]], Op.is_gt, 0, -1)
+    iota(a("i2"), [[256, 16], [1, 128]], 0, 0)
+    fill(a("z1"), 0.0)
+    fill(a("zf"), 0.0)
+    fill(a("xt0", 2048, 2304), 0.0)
+    fill(a("xt1", 2048, 2304), 0.0)
+    ts(a("li"), a("pi"), 15, Op.bitwise_and)
+    copy(a("lf"), a("li"))
+    copy(a("z1", 15, 143, 16), a("gm", 0, 128, 16))
+    ts(a("z64"), a("z1"), 64.0, Op.mult)
+    fill(a("rst"), 0.0)
+    fill(a("rst", 0, 256, 16), 1000000.0)
+    fill(a("thr"), 65536.0)
+    fill(a("aa"), 0)
+    fill(a("wt", 0, 1536), 0.0)
+    copy(a("p16_0"), a("np_"))
+    for h in range(2):
+        copy(a("k16_0_%d" % h), a("nk", 128 * h, 128 * h + 128))
+    ts(a("kp"), a("nk"), 32.0, Op.add)
+    tt(a("l3"), a("lz"), a("ls"), Op.mult)
+    tt(a("l4"), a("l3"), a("lk"), Op.add)
+    ts(a("l5"), a("l4"), 15, Op.bitwise_and)
+    ts(a("lutf"), a("l5"), a("lf", 0, 1), Op.is_equal)
+    ts(a("lutk"), a("lk"), a("lf", 0, 1), Op.is_equal)
+    fill(a("wt", 1536, 4096), 0.0)
+    copy(a("p32"), a("np_"))
+    waits("y", need("dma", [], [a("zf")]))
+    g.sync.dma_start(T.kd[:, 0, :], T.zf[0:8, :]).then_inc(T.sem["kz"], 16)
+    g.sync.wait_ge(T.sem["kz"], 16)
+
+    def consts2():
+        fill(a("lutm"), 32.0)
+        fill(a("lutm", 2, 3), 4096.0)
+        fill(a("luto"), 4096.0)
+        fill(a("luto", 1, 2), 0.0)
+        fill(a("lutp"), 0.0)
+        ts(a("lutp", 1, 2), a("lf", 0, 1), 0.0, Op.is_equal)
+        fill(a("zero"), 0.0)
+        fill(a("rs2"), -256.0)
+        fill(a("rs2", 0, 256, 16), 1000000.0)
+        copy(a("pf"), a("pi"))
+        ts(a("pl", 0, 1), a("lf", 0, 1), 256.0, Op.mult, a("pf", 0, 1), Op.add)
+        ts(a("cf"), a("q16"), a("lf", 0, 1), Op.add)
+        ts(a("c16"), a("cf"), 16.0, Op.mult)
+        ts(a("cd"), a("cf"), 2048.0, Op.add)
+        ts(a("cw"), a("cf"), 7936.0, Op.add)
+        ts(a("dg_"), a("i2"), a("pl", 0, 1), Op.is_equal)
+
+    def lanes(out, z, src, c, first):
+        for i in range(16):
+            mm(out, a(z, 15 - i, 143 - i), a3(src, 4 * c, 4 * c + 4, 16 * i, 16 * i + 16), first and i == 0, i == 15)
+
+    dmas = {"kd": 0, "wd": 0}
+
+    def next_table(t):
+        x, n = "xt%d" % (t % 2), "xt%d" % ((t + 1) % 2)
+        dma("y", "xc%d" % t, T[n][:, 0:2048], T[x][:, 0:2048], [a(n, 0, 2048)], [a(x, 0, 2048)])
+
+    def shifted():
+        y, w, k = g.sync, "wd", "kd"
+
+        def start(sem, out, in_):
+            y.dma_start(out, in_).then_inc(T.sem[sem], 16)
+            dmas[sem] += 16
+
+        if dmas[w]:
+            waits("y", {w: dmas[w]})
+        waits("y", need("dma", [], [a("kp")]))
+        start(k, T.kd[:, 1:17, :], T.kp[:])
+        for r in range(15):
+            start(k, T.kd[:, 17 + r, :], T.kp[15:128:16, :])
+        note("dma", k, dmas[k], [], [a("kp")], {})
+        waits("y", need("dma", [a("wt")], []))
+        start(w, T.wt[:, 7936:8192], T.kp[:])
+        y.wait_ge(T.sem[k], dmas[k])
+        for j in range(1, 16):
+            start(w, T.wt[j:128:16, 0:4096], T.kd[:, 1 + j:17 + j, :])
+        start(w, T.wt[:, 4096:4352], T.kd[:, 0:16, :])
+        note("dma", w, dmas[w], [a("wt")], [a("kp")], {})
+
+    sent = [0]
+    nxt, prv = T.cores[(rank + 1) % n_ranks], T.cores[(rank - 1) % n_ranks]
+    n_k = len(topo.engines(prv, core))
+    n_p = len(topo.engines(nxt, core))
+
+    def send(name, dst_name, dst, sem, n_in):
+        rid, pid = topo.addr(dst, core)
+        waits("g", need("g", [], [a(name)]))
+        g.remote_dma(T[dst_name][:], T[name][:], T.sem[sem], T.sem["sent"], pid, rid, topo.mask(core, dst))
+        sent[0] += len(topo.engines(core, dst))
+        note("dma", sem, n_in, [a(dst_name)], [], {})
+
+    def gather_y(t, c):
+        act(a("yg", 1024 * c, 1024 * c + 1024), ind(a("xt%d" % (t % 2)), a("p16_%d" % t, 64 * c, 64 * c + 64)), AF.Copy)
+
+    for t in range(RO):
+        last, first = t == RO - 1, t == 0
+        xt, xn = "xt%d" % (t % 2), "xt%d" % ((t + 1) % 2)
+
+        def d_chunk(t, c):
+            for q in range(4 * c, 4 * c + 4):
+                tt(row("d3", q), ind(a("xt%d" % (t % 2)), a("k16_%d_%d" % (t, q // 8), 16 * (q % 8), 16 * (q % 8) + 16)),
+                   a("yg", 256 * q, 256 * q + 256), Op.subtract)
+
+        def d_abs(c):
+            act(a3("a3", 4 * c, 4 * c + 4), a3("d3", 4 * c, 4 * c + 4), AF.Abs)
+
+        def t_sum(c):
+            lanes(a(("bT", "bT2")[c // 2], 64 * c, 64 * c + 64), "z1", "d3", c, True)
+
+        def d_sum(c):
+            o = a(("bD", "bD2")[c // 2], 64 * c, 64 * c + 64)
+            mm(o, a("idn"), a("cj", 64 * c, 64 * c + 64), True, False)
+            lanes(o, "z64", "a3", c, False)
+
+        def sign(h):
+            s = (128 * h, 128 * h + 128)
+            act(a("sn", *s), a(("bT", "bT2")[h], *s), AF.Sign)
+
+        def s_gather(c):
+            lo = 64 * (c % 2)
+            act(a("sg", 1024 * c, 1024 * c + 1024), ind(a(xt), a("k16_%d_%d" % (t, c // 2), lo, lo + 64)), AF.Copy)
+
+        def least(h):
+            s, m = (128 * h, 128 * h + 128), (8 * h, 8 * h + 8)
+            tt(a("code", *s), a(("bD", "bD2")[h], *s), a("sn", *s), Op.add)
+            scan(a("mi", *s), a("rst", *s), a("code", *s), Op.max, Op.min)
+            ts(a("v8", *m), a("mi", s[0] + 15, s[1], 16), 255, Op.bitwise_and)
+            copy(a("l8", *m), a("v8", *m))
+            tt(a("nsel", *s), ind(a("lutf"), a("l8", *m)), a("p32", *s), Op.mult)
+            mm(a("bN", *s), a("gm"), a("nsel", *s), True, True)
+
+        def heads(h):
+            copy(a("nb", 128 * h, 128 * h + 128), a("bN", 128 * h, 128 * h + 128))
+
+        def plus(t, h):
+            ts(a("kp", 128 * h, 128 * h + 128), a("k16_%d_%d" % (t, h)), 32.0, Op.add)
+
+        def near(c):
+            s = (1024 * c, 1024 * c + 1024)
+            tt(a("eg", *s), ind(a(xt), a("nb", 64 * c, 64 * c + 64)), a("sg", *s), Op.subtract)
+
+        def near_abs(c):
+            act(a3("ae", 4 * c, 4 * c + 4), a("eg", 1024 * c, 1024 * c + 1024), AF.Abs)
+            lanes(a(("bD", "bD2")[c // 2], 64 * c, 64 * c + 64), "z1", "ae", c, True)
+
+        def arrays(h):
+            s, m = (128 * h, 128 * h + 128), (8 * h, 8 * h + 8)
+            ts(a("ew", *s), a(("bD", "bD2")[h], *s), 1040.0, Op.is_lt, -4096.0, Op.mult)
+            scan(a("ms", *s), a("rs2", *s), a("ew", *s), Op.add, Op.min)
+            tt(a("o1", *m), a("ms", s[0] + 15, s[1], 16), a("npx", *m), Op.max)
+            tt(a("o2", *m), a("o1", *m), a("cw", *m), Op.add)
+            copy(a("o16", *m), a("o2", *m))
+            tt(a("fr", *s), ind(a("wt"), a("o16", *m)), a("nfix", *s), Op.add)
+            if last:
+                ts(a("yk32", *s), a("fr", *s), -32.0, Op.add)
+            else:
+                ts(a("ks_%d_%d" % (t, h)), a("fr", *s), -32.0, Op.add)
+                send("ks_%d_%d" % (t, h), "k16_%d_%d" % (t + 1, h), nxt, "ka%d_%d" % (t + 1, h), n_k)
+
+        def fates():
+            mc = a("mi", 15, 256, 16)
+            ts(a("lt"), mc, a("thr"), Op.is_lt)
+            ts(a("kf"), mc, 53248.0, Op.is_lt)
+            tt(a("ksel"), ind(a("lutk"), a("l8")), a("p32"), Op.mult)
+            mm(a("bM", 32, 48), a("gm"), a("kf"), True, True)
+            mm(a("bT2", 0, 256), a("gm"), a("ksel"), True, True)
+            tt(a("fl"), a("lt"), a("kf"), Op.add)
+            copy(a("fl16"), a("fl"))
+
+        def names():
+            act(a("pks"), a("bT2", 0, 256), AF.Copy)
+            act(a("ns"), a("bN", 0, 256), AF.Copy, bias=32.0)
+
+        def phages():
+            tt(a("pa"), ind(a("lutm"), a("fl16")), a("kp"), Op.min)
+            ts(a("kk"), a("v8"), 2, Op.logical_shift_right, 15, Op.bitwise_and)
+            tt(a("pt"), a("pa"), a("p32"), Op.mult)
+            tt(a("ok"), a("kk"), a("c16"), Op.add)
+            ts(a("pn"), a("pt"), 5, Op.logical_shift_right, 2047, Op.bitwise_and)
+            copy(a("ok16"), a("ok"))
+            if last:
+                copy(a("yp32"), a("pn"))
+                dma("y", "op", T.yp[:], T.yp32[:], [], [a("yp32")])
+            else:
+                copy(a("ps_%d" % t), a("pn"))
+                send("ps_%d" % t, "p16_%d" % (t + 1), prv, "pa%d" % (t + 1), n_p)
+            act(a("yk_"), ind(a("yg"), a("ok16")), AF.Copy)
+            act(a("sgn"), ind(a("yg"), a("ok16")), AF.Sign, scale=-1.0, bias=127.5)
+
+        def writers():
+            tt(a("rr"), ind(a("luto"), a("fl16")), a("pks"), Op.max)
+            for i in range(16):
+                mm(a("bM", 0, 16), a("dg_", 128 * i, 128 * i + 128), a("rr", i, 256, 16), i == 0, i == 15)
+
+        def values():
+            tt(a("dk"), ind(a("sg"), a("ok16")), a("yk_"), Op.subtract)
+            act(a("adk"), a("dk"), AF.Abs)
+            tt(a("nfix"), ind(a("lutp"), a("fl16")), a("ns"), Op.mult)
+            ts(a("npx"), a("fl"), 1.0, Op.is_equal, -8192.0, Op.mult)
+
+        def equals():
+            copy(a("ol"), a("bM", 0, 16))
+            for q in range(16):
+                ts(a("eq", 272 * q, 256 * q + 256), a("rr", 16 * q, 256), a("ol", q, q + 1), Op.is_equal)
+                mm(a("bC", 16 * q, 16 * q + 16), a("tri"), a("eq", 272 * q, 272 * q + 16), q == 0, q in (0, 15))
+                if q < 15:
+                    mm(a("bC", 16 * q + 16, 256), a("gm"), a("eq", 272 * q + 16, 256 * q + 256), q == 0, False)
+
+        def counts():
+            act(a("cs"), a("bC", 0, 256), AF.Copy, scale=4096.0)
+            for i in range(16):
+                mm(a("bM", 16, 32), a("dg_", 128 * i, 128 * i + 128), a("cs", i, 256, 16), i == 0, i == 15)
+
+        def change():
+            ts(a("c1"), a("adk"), 32.0, Op.is_le, 128.0, Op.mult)
+            tt(a("tt"), a("c1"), a("sgn"), Op.mult)
+
+        def scatter():
+            tt(a("v1"), a("bM", 16, 32), a("ol"), Op.add)
+            tt(a("v2"), a("v1"), a("cd"), Op.min)
+            copy(a("w16"), a("v2"))
+            tt(ind(a(xn), a("w16")), a("yk_"), a("tt"), Op.add)
+
+        def allowance():
+            do("v", lambda: V.tensor_reduce(T.ca[:], T.bM[:, 32:48], AX.X, Op.add), [a("ca")], [a("bM", 32, 48)])
+            tt(a("aa"), a("aa"), a("ca"), Op.add)
+            ts(a("ab"), a("aa"), 15, Op.bitwise_and)
+            ts(a("thr"), a("ab"), 256.0, Op.mult, 65536.0, Op.add)
+
+        next_table(t)
+        if first:
+            shifted()
+            for c in range(4):
+                gather_y(0, c)
+            d_chunk(0, 0)
+        t_sum(0)
+        d_abs(0)
+        d_sum(0)
+        s_gather(0)
+        d_chunk(t, 1)
+        if not first:
+            plus(t, 1)
+            shifted()
+        t_sum(1)
+        d_abs(1)
+        sign(0)
+        d_sum(1)
+        d_chunk(t, 2)
+        d_abs(2)
+        t_sum(2)
+        s_gather(1)
+        d_chunk(t, 3)
+        d_abs(3)
+        least(0)
+        d_sum(2)
+        t_sum(3)
+        sign(1)
+        d_sum(3)
+        if first:
+            consts2()
+        heads(0)
+        near(0)
+        near(1)
+        least(1)
+        fates()
+        heads(1)
+        near_abs(0)
+        s_gather(2)
+        names()
+        near(2)
+        writers()
+        s_gather(3)
+        near_abs(1)
+        phages()
+        equals()
+        values()
+        counts()
+        near_abs(2)
+        change()
+        if not last:
+            allowance()
+            copy(a("p32"), a("p16_%d" % (t + 1)))
+        arrays(0)
+        scatter()
+        near(3)
+        if last:
+            dma("y", "oy", T.yx[:], T[xn][:, 0:2048], [], [a(xn, 0, 2048)])
+        else:
+            gather_y(t + 1, 0)
+        near_abs(3)
+        if not last:
+            for c in range(1, 4):
+                gather_y(t + 1, c)
+            plus(t + 1, 0)
+            d_chunk(t + 1, 0)
+        arrays(1)
+        if last:
+            dma("y", "ok", T.yk[:], T.yk32[:], [], [a("yk32")])
+    g.wait_ge(T.sem["sent"], sent[0])
+    for s in ("oy", "ok", "op"):
+        g.sync.wait_ge(T.sem[s], 16)
+    for q in cnt:
+        if seen["y"].get(q, 0) < cnt[q]:
+            g.sync.wait_ge(T.sem[q], cnt[q])

@@ -9,28 +9,31 @@ for _n, _w, _d in (
         ("v8", 16, I), ("l8", 16, U), ("kf", 16, B), ("lt", 16, F), ("fl", 16, F), ("fl16", 16, U),
         ("nsel", 256, H), ("ksel", 256, H), ("nb", 256, U), ("ns", 256, F), ("pks", 256, F),
         ("pa", 256, F), ("pt", 256, I), ("pn", 256, I), ("yp32", 256, F),
-        ("npx", 16, F), ("o1", 16, F), ("o2", 16, F), ("o16", 16, U), ("nfix", 256, F), ("wt", 8192, F), ("fr", 256, F),
+        ("npx", 16, F), ("o1", 16, F), ("o2", 16, F), ("o16", 16, U), ("nfix", 256, F), ("kh", 128, H),
+        ("wt0", 4096, F), ("wt1", 4096, F), ("fr", 256, F),
         ("yk32", 256, F), ("ew", 256, F), ("ms", 256, F), ("zf", 256, F),
         ("rr", 256, H), ("ol", 16, F), ("eq", 4096, B), ("cs", 256, B), ("v1", 16, F), ("v2", 16, F), ("w16", 16, U),
         ("kk", 16, I), ("ok", 16, I), ("ok16", 16, U), ("yk_", 256, B), ("dk", 256, B), ("adk", 256, B), ("sgn", 256, B),
         ("c1", 256, B), ("tt", 256, B), ("ca", 1, F), ("aa", 1, I), ("ab", 1, I), ("thr", 1, F),
-        ("pi", 2, I), ("li", 2, I), ("lf", 2, F), ("pf", 2, F), ("pl", 2, F), ("i2", 2048, I),
+        ("pi", 2, I), ("li", 2, I), ("lf", 2, F), ("pf", 2, F), ("pl", 2, F), ("i1", 2048, I), ("i2", 2048, I), ("st", 2048, B),
         ("dg_", 2048, B), ("ones", 128, B), ("gm", 128, B), ("tri", 128, B), ("idn", 128, B),
-        ("z1", 143, B), ("z64", 143, B), ("cj", 256, B), ("rst", 256, F), ("rs2", 256, F), ("zero", 256, B),
+        ("z1", 143, B), ("z64", 143, B), ("cj", 256, B), ("rst", 256, F), ("rs2", 256, F),
         ("q16", 16, F), ("cf", 16, F), ("c16", 16, I), ("cd", 16, F), ("cw", 16, F),
-        ("lk", 256, I), ("lz", 256, I), ("ls", 256, I), ("l3", 256, I), ("l4", 256, I), ("l5", 256, I),
+        ("lk", 256, I), ("lz", 256, I), ("ls", 256, I), ("l3", 256, I),
         ("lutf", 256, B), ("lutk", 256, B), ("lutm", 16, F), ("luto", 16, F), ("lutp", 16, F)):
     SCRATCH[_n] = ("sbuf", [128, _w], _d)
 for _n in ("d3", "a3", "ae"):
     SCRATCH[_n] = ("sbuf", [128, 16, 256], B)
-SCRATCH["kd"] = ("dram", [8, 32, 256], F)
+SCRATCH["kd"] = ("dram", [8, 32, 128], F)
 for _t in range(RO):
     for _h in range(2):
         SCRATCH["k16_%d_%d" % (_t, _h)] = ("sbuf", [128, 128], U)
         SCRATCH["ks_%d_%d" % (_t, _h)] = ("sbuf", [128, 128], U)
     SCRATCH["p16_%d" % _t] = ("sbuf", [128, 256], U)
     SCRATCH["ps_%d" % _t] = ("sbuf", [128, 256], U)
-PSUM = ("bT", "bT2", "bD", "bD2", "bN", "bM", "bC")
+ORDER = """ts0 da0 dc2 ts1 da1 sn0 ds0 ds1 sg0 dc3 ts2 le0 pl1 ts3 he0 sg1 da2 da3 ds2 sn1 n0 ds3 na0 sg2 n1 le1 fa he1 pk kh n2 nl0
+    sh0 sg3 sh1 wr ph sh2 eq yk al na1 nl1 n3 va ar0 co na2 na3 sh3 sh4 nl2 ch sc y0 y1 nl3 y2 p32 y3 ar1 pl0 dc0 dc1 w0"""
+PSUM = ("bT", "bT2", "bD", "bD2", "bN", "bM", "bC", "bZ")
 for _n in PSUM:
     SCRATCH[_n] = ("psum", [128, 512], F)
 SEMAPHORES = (["v", "s", "p", "g", "lx", "lp", "lk", "oy", "ok", "op", "sent", "kz", "kd", "wd"]
@@ -162,6 +165,7 @@ def rank_program(g, core, T, topo):
     iota(a("ls"), [[0, 64], [2, 2], [0, 2]], -1, 0)
     iota(a("q16"), [[16, 16]], 0, 0, **small)
     asel(a("tri"), a("gm"), [[1, 128]], Op.is_gt, 0, -1)
+    iota(a("i1"), [[1, 16], [0, 8], [1, 16]], -1, 0)
     iota(a("i2"), [[256, 16], [1, 128]], 0, 0)
     fill(a("z1"), 0.0)
     fill(a("zf"), 0.0)
@@ -175,21 +179,26 @@ def rank_program(g, core, T, topo):
     fill(a("rst", 0, 256, 16), 1000000.0)
     fill(a("thr"), 65536.0)
     fill(a("aa"), 0)
-    fill(a("wt", 0, 1536), 0.0)
+    fill(a("wt0", 0, 2048), 0.0)
     copy(a("p16_0"), a("np_"))
     for h in range(2):
         copy(a("k16_0_%d" % h), a("nk", 128 * h, 128 * h + 128))
     ts(a("kp"), a("nk"), 32.0, Op.add)
     tt(a("l3"), a("lz"), a("ls"), Op.mult)
-    tt(a("l4"), a("l3"), a("lk"), Op.add)
-    ts(a("l5"), a("l4"), 15, Op.bitwise_and)
-    ts(a("lutf"), a("l5"), a("lf", 0, 1), Op.is_equal)
+    tt(a("lz"), a("l3"), a("lk"), Op.add)
+    ts(a("l3"), a("lz"), 15, Op.bitwise_and)
+    ts(a("lutf"), a("l3"), a("lf", 0, 1), Op.is_equal)
     ts(a("lutk"), a("lk"), a("lf", 0, 1), Op.is_equal)
-    fill(a("wt", 1536, 4096), 0.0)
     copy(a("p32"), a("np_"))
     waits("y", need("dma", [], [a("zf")]))
-    g.sync.dma_start(T.kd[:, 0, :], T.zf[0:8, :]).then_inc(T.sem["kz"], 16)
+    g.sync.dma_start(T.kd[:, 0, :], T.zf[0:8, 0:128]).then_inc(T.sem["kz"], 16)
     g.sync.wait_ge(T.sem["kz"], 16)
+
+    def consts1():
+        ts(a("st"), a("i1"), 15.0, Op.min, a("lf", 0, 1), Op.is_equal)
+        fill(a("st", 0, 2048, 16), 0.0)
+        asel(a("st"), a("st"), [[0, 16], [-16, 8], [0, 16]], Op.is_ge, 0, 1)
+        asel(a("st"), a("st"), [[0, 16], [16, 8], [0, 16]], Op.is_ge, 15, -1)
 
     def consts2():
         fill(a("lutm"), 32.0)
@@ -198,15 +207,15 @@ def rank_program(g, core, T, topo):
         fill(a("luto", 1, 2), 0.0)
         fill(a("lutp"), 0.0)
         ts(a("lutp", 1, 2), a("lf", 0, 1), 0.0, Op.is_equal)
-        fill(a("zero"), 0.0)
-        fill(a("rs2"), -256.0)
+        fill(a("rs2"), -128.0)
         fill(a("rs2", 0, 256, 16), 1000000.0)
         copy(a("pf"), a("pi"))
         ts(a("pl", 0, 1), a("lf", 0, 1), 256.0, Op.mult, a("pf", 0, 1), Op.add)
         ts(a("cf"), a("q16"), a("lf", 0, 1), Op.add)
         ts(a("c16"), a("cf"), 16.0, Op.mult)
         ts(a("cd"), a("cf"), 2048.0, Op.add)
-        ts(a("cw"), a("cf"), 7936.0, Op.add)
+        ts(a("cw", 0, 8), a("cf", 0, 8), 3968.0, Op.add)
+        ts(a("cw", 8, 16), a("cf", 8, 16), 3840.0, Op.add)
         ts(a("dg_"), a("i2"), a("pl", 0, 1), Op.is_equal)
 
     def lanes(out, z, src, c, first):
@@ -219,7 +228,18 @@ def rank_program(g, core, T, topo):
         x, n = "xt%d" % (t % 2), "xt%d" % ((t + 1) % 2)
         dma("y", "xc%d" % t, T[n][:, 0:2048], T[x][:, 0:2048], [a(n, 0, 2048)], [a(x, 0, 2048)])
 
-    def shifted():
+    def shifted1(k):
+        z = ("bT", "bZ")[k % 2]
+        for u in range(4 * k, min(4 * k + 4, 18)):
+            o, s = 128 * (u - 4 * k), 0 if u == 16 else 128 * min(u + 1, 15)
+            mm(a(z, o, o + 128), a("idn") if u == 17 else a("st", s, s + 128), a("kh"), True, True)
+        if k < 4:
+            act(a("wt1", 512 * k, 512 * k + 512), a(z), AF.Copy)
+        else:
+            act(a("wt1", 2048, 2176), a(z, 0, 128), AF.Copy)
+            act(a("wt1", 3968, 4096), a(z, 128, 256), AF.Copy)
+
+    def shifted0():
         y, w, k = g.sync, "wd", "kd"
 
         def start(sem, out, in_):
@@ -228,18 +248,19 @@ def rank_program(g, core, T, topo):
 
         if dmas[w]:
             waits("y", {w: dmas[w]})
-        waits("y", need("dma", [], [a("kp")]))
-        start(k, T.kd[:, 1:17, :], T.kp[:])
+        kp = a("kp", 0, 128)
+        waits("y", need("dma", [], [kp]))
+        start(k, T.kd[:, 1:17, :], kp[0])
         for r in range(15):
-            start(k, T.kd[:, 17 + r, :], T.kp[15:128:16, :])
-        note("dma", k, dmas[k], [], [a("kp")], {})
-        waits("y", need("dma", [a("wt")], []))
-        start(w, T.wt[:, 7936:8192], T.kp[:])
+            start(k, T.kd[:, 17 + r, :], T.kp[15:128:16, 0:128])
+        note("dma", k, dmas[k], [], [kp], {})
+        waits("y", need("dma", [a("wt0")], []))
+        start(w, T.wt0[:, 3968:4096], kp[0])
         y.wait_ge(T.sem[k], dmas[k])
         for j in range(1, 16):
-            start(w, T.wt[j:128:16, 0:4096], T.kd[:, 1 + j:17 + j, :])
-        start(w, T.wt[:, 4096:4352], T.kd[:, 0:16, :])
-        note("dma", w, dmas[w], [a("wt")], [a("kp")], {})
+            start(w, T.wt0[j:128:16, 0:2048], T.kd[:, 1 + j:17 + j, :])
+        start(w, T.wt0[:, 2048:2176], T.kd[:, 0:16, :])
+        note("dma", w, dmas[w], [a("wt0")], [kp], {})
 
     sent = [0]
     nxt, prv = T.cores[(rank + 1) % n_ranks], T.cores[(rank - 1) % n_ranks]
@@ -299,26 +320,33 @@ def rank_program(g, core, T, topo):
         def plus(t, h):
             ts(a("kp", 128 * h, 128 * h + 128), a("k16_%d_%d" % (t, h)), 32.0, Op.add)
 
+        def half1():
+            copy(a("kh"), a("k16_%d_1" % t))
+
         def near(c):
             s = (1024 * c, 1024 * c + 1024)
             tt(a("eg", *s), ind(a(xt), a("nb", 64 * c, 64 * c + 64)), a("sg", *s), Op.subtract)
 
         def near_abs(c):
             act(a3("ae", 4 * c, 4 * c + 4), a("eg", 1024 * c, 1024 * c + 1024), AF.Abs)
+
+        def near_sum(c):
             lanes(a(("bD", "bD2")[c // 2], 64 * c, 64 * c + 64), "z1", "ae", c, True)
 
         def arrays(h):
             s, m = (128 * h, 128 * h + 128), (8 * h, 8 * h + 8)
-            ts(a("ew", *s), a(("bD", "bD2")[h], *s), 1040.0, Op.is_lt, -4096.0, Op.mult)
+            ts(a("ew", *s), a(("bD", "bD2")[h], *s), 1040.0, Op.is_lt, -2048.0, Op.mult)
             scan(a("ms", *s), a("rs2", *s), a("ew", *s), Op.add, Op.min)
             tt(a("o1", *m), a("ms", s[0] + 15, s[1], 16), a("npx", *m), Op.max)
             tt(a("o2", *m), a("o1", *m), a("cw", *m), Op.add)
             copy(a("o16", *m), a("o2", *m))
-            tt(a("fr", *s), ind(a("wt"), a("o16", *m)), a("nfix", *s), Op.add)
-            if last:
-                ts(a("yk32", *s), a("fr", *s), -32.0, Op.add)
+            tt(a("fr", *s), ind(a("wt%d" % h), a("o16", *m)), a("nfix", *s), Op.add)
+            out = a("yk32", *s) if last else a("ks_%d_%d" % (t, h))
+            if h == 0:
+                ts(out, a("fr", *s), -32.0, Op.add)
             else:
-                ts(a("ks_%d_%d" % (t, h)), a("fr", *s), -32.0, Op.add)
+                copy(out, a("fr", *s))
+            if not last:
                 send("ks_%d_%d" % (t, h), "k16_%d_%d" % (t + 1, h), nxt, "ka%d_%d" % (t + 1, h), n_k)
 
         def fates():
@@ -333,7 +361,8 @@ def rank_program(g, core, T, topo):
 
         def names():
             act(a("pks"), a("bT2", 0, 256), AF.Copy)
-            act(a("ns"), a("bN", 0, 256), AF.Copy, bias=32.0)
+            act(a("ns", 0, 128), a("bN", 0, 128), AF.Copy, bias=32.0)
+            act(a("ns", 128, 256), a("bN", 128, 256), AF.Copy)
 
         def phages():
             tt(a("pa"), ind(a("lutm"), a("fl16")), a("kp"), Op.min)
@@ -348,6 +377,8 @@ def rank_program(g, core, T, topo):
             else:
                 copy(a("ps_%d" % t), a("pn"))
                 send("ps_%d" % t, "p16_%d" % (t + 1), prv, "pa%d" % (t + 1), n_p)
+
+        def lanes_k():
             act(a("yk_"), ind(a("yg"), a("ok16")), AF.Copy)
             act(a("sgn"), ind(a("yg"), a("ok16")), AF.Sign, scale=-1.0, bias=127.5)
 
@@ -393,71 +424,33 @@ def rank_program(g, core, T, topo):
 
         next_table(t)
         if first:
-            shifted()
+            shifted0()
             for c in range(4):
                 gather_y(0, c)
             d_chunk(0, 0)
-        t_sum(0)
-        d_abs(0)
-        d_sum(0)
-        s_gather(0)
-        d_chunk(t, 1)
+            d_chunk(0, 1)
+        steps = {"le0": lambda: (consts1() if first else None, least(0)), "le1": lambda: least(1),
+                 "he0": lambda: (consts2() if first else None, heads(0)), "he1": lambda: heads(1),
+                 "dc2": lambda: d_chunk(t, 2), "dc3": lambda: d_chunk(t, 3), "sn0": lambda: sign(0), "sn1": lambda: sign(1),
+                 "fa": fates, "pk": names, "kh": half1, "wr": writers, "ph": phages, "yk": lanes_k, "eq": equals, "va": values,
+                 "co": counts, "ch": change, "sc": scatter, "ar0": lambda: arrays(0), "ar1": lambda: arrays(1)}
+        for c in range(4):
+            for x, f in (("ts", t_sum), ("da", d_abs), ("ds", d_sum), ("sg", s_gather), ("n", near), ("na", near_abs), ("nl", near_sum)):
+                steps["%s%d" % (x, c)] = lambda f=f, c=c: f(c)
+        for k in range(5):
+            steps["sh%d" % k] = lambda k=k: shifted1(k)
         if not first:
-            plus(t, 1)
-            shifted()
-        t_sum(1)
-        d_abs(1)
-        sign(0)
-        d_sum(1)
-        d_chunk(t, 2)
-        d_abs(2)
-        t_sum(2)
-        s_gather(1)
-        d_chunk(t, 3)
-        d_abs(3)
-        least(0)
-        d_sum(2)
-        t_sum(3)
-        sign(1)
-        d_sum(3)
-        if first:
-            consts2()
-        heads(0)
-        near(0)
-        near(1)
-        least(1)
-        fates()
-        heads(1)
-        near_abs(0)
-        s_gather(2)
-        names()
-        near(2)
-        writers()
-        s_gather(3)
-        near_abs(1)
-        phages()
-        equals()
-        values()
-        counts()
-        near_abs(2)
-        change()
+            steps["pl1"] = lambda: plus(t, 1)
         if not last:
-            allowance()
-            copy(a("p32"), a("p16_%d" % (t + 1)))
-        arrays(0)
-        scatter()
-        near(3)
-        if last:
-            dma("y", "oy", T.yx[:], T[xn][:, 0:2048], [], [a(xn, 0, 2048)])
-        else:
-            gather_y(t + 1, 0)
-        near_abs(3)
-        if not last:
-            for c in range(1, 4):
-                gather_y(t + 1, c)
-            plus(t + 1, 0)
-            d_chunk(t + 1, 0)
-        arrays(1)
+            steps.update({"al": allowance, "p32": lambda: copy(a("p32"), a("p16_%d" % (t + 1))), "pl0": lambda: plus(t + 1, 0),
+                          "w0": shifted0, "dc0": lambda: d_chunk(t + 1, 0), "dc1": lambda: d_chunk(t + 1, 1)})
+            for c in range(4):
+                steps["y%d" % c] = lambda c=c: gather_y(t + 1, c)
+        for x in ORDER.split():
+            if x in steps:
+                steps[x]()
+            if x == "sc" and last:
+                dma("y", "oy", T.yx[:], T[xn][:, 0:2048], [], [a(xn, 0, 2048)])
         if last:
             dma("y", "ok", T.yk[:], T.yk32[:], [], [a("yk32")])
     g.wait_ge(T.sem["sent"], sent[0])

from concourse.mybir import AluOpType as Op, ActivationFunctionType as AF, AxisListType as AX

RO = 4
F, B, H, I, U = "float32", "bfloat16", "float16", "int32", "uint16"
SCRATCH = {}
for _n, _w, _d in (
        ("xt0", 2304, B), ("xt1", 2304, B), ("nk", 256, I), ("np_", 256, I), ("yg", 4096, B), ("sg", 4096, B), ("eg", 4096, B),
        ("kp", 256, F), ("p32", 256, F), ("sn", 256, F), ("code", 256, F), ("mi", 256, I),
        ("v8", 16, I), ("l8", 16, U), ("kf", 16, B), ("lt", 16, F), ("fl", 16, F), ("fl16", 16, U),
        ("nsel", 256, H), ("ksel", 256, H), ("nb", 256, U), ("ns", 256, F), ("pks", 256, F),
        ("pa", 256, F), ("pt", 256, I), ("pn", 256, I), ("yp32", 256, F),
        ("npx", 16, F), ("o1", 16, F), ("o2", 16, F), ("o16", 16, U), ("nfix", 256, F), ("kh", 128, H),
        ("wt0", 4096, F), ("wt1", 4096, F), ("fr", 256, F),
        ("yk32", 256, F), ("ew", 256, F), ("ms", 256, F), ("zf", 256, F),
        ("rr", 256, H), ("ol", 16, F), ("eq", 4096, B), ("cs", 256, B), ("v1", 16, F), ("v2", 16, F), ("w16", 16, U),
        ("kk", 16, I), ("ok", 16, I), ("ok16", 16, U), ("yk_", 256, B), ("dk", 256, B), ("adk", 256, B), ("sgn", 256, B),
        ("c1", 256, B), ("tt", 256, B), ("ca", 1, F), ("aa", 1, I), ("ab", 1, I), ("thr", 1, F),
        ("pi", 2, I), ("li", 2, I), ("lf", 2, F), ("pf", 2, F), ("pl", 2, F), ("i1", 2048, I), ("i2", 2048, I), ("st", 2048, B),
        ("dg_", 2048, B), ("ones", 128, B), ("gm", 128, B), ("tri", 128, B), ("idn", 128, B),
        ("z1", 143, B), ("z64", 143, B), ("cj", 256, B), ("rst", 256, F), ("rs2", 256, F),
        ("q16", 16, F), ("cf", 16, F), ("c16", 16, I), ("cd", 16, F), ("cw", 16, F),
        ("lk", 256, I), ("lz", 256, I), ("ls", 256, I), ("l3", 256, I),
        ("lutf", 256, B), ("lutk", 256, B), ("lutm", 16, F), ("luto", 16, F), ("lutp", 16, F)):
    SCRATCH[_n] = ("sbuf", [128, _w], _d)
for _n in ("d3", "a3", "ae"):
    SCRATCH[_n] = ("sbuf", [128, 16, 256], B)
SCRATCH["kd"] = ("dram", [8, 32, 128], F)
for _t in range(RO):
    for _h in range(2):
        SCRATCH["k16_%d_%d" % (_t, _h)] = ("sbuf", [128, 128], U)
        SCRATCH["ks_%d_%d" % (_t, _h)] = ("sbuf", [128, 128], U)
    SCRATCH["p16_%d" % _t] = ("sbuf", [128, 256], U)
    SCRATCH["ps_%d" % _t] = ("sbuf", [128, 256], U)
ORDER = """ts0 da0 dc2 ts1 da1 sn0 ds0 ds1 sg0 dc3 ts2 le0 pl1 ts3 he0 sg1 da2 da3 ds2 sn1 n0 ds3 na0 sg2 n1 le1 fa he1 pk kh n2 nl0
    sh0 sg3 sh1 wr ph sh2 eq yk al na1 nl1 n3 va ar0 co na2 na3 sh3 sh4 nl2 ch sc y0 y1 nl3 y2 p32 y3 ar1 pl0 dc0 dc1 w0"""
PSUM = ("bT", "bT2", "bD", "bD2", "bN", "bM", "bC", "bZ")
for _n in PSUM:
    SCRATCH[_n] = ("psum", [128, 512], F)
SEMAPHORES = (["v", "s", "p", "g", "lx", "lp", "lk", "oy", "ok", "op", "sent", "kz", "kd", "wd"]
              + ["ka%d_%d" % (t, h) for t in range(1, RO) for h in range(2)] + ["pa%d" % t for t in range(1, RO)]
              + ["xc%d" % t for t in range(RO)])


def rank_program(g, core, T, topo):
    rank = T.rank_of(core)
    if rank is None:
        return
    n_ranks = len(T.cores)
    Q = {"v": g.vector, "s": g.scalar, "p": g.tensor, "g": g, "y": g.sync}
    cnt = {"v": 0, "s": 0, "p": 0, "g": 0}
    seen = {q: {} for q in Q}
    snap, hist = {}, {}

    def a(name, lo=0, hi=None, step=None):
        hi = SCRATCH[name][1][1] if hi is None else hi
        return (T[name][:, lo:hi] if step is None else T[name][:, lo:hi:step], name, lo, hi)

    def a3(name, q0, q1, c0=None, c1=None):
        return (T[name][:, q0:q1, :] if c0 is None else T[name][:, q0:q1, c0:c1], name, 256 * q0, 256 * q1)

    def row(name, q):
        return (T[name][:, q], name, 256 * q, 256 * q + 256)

    def ind(win, off):
        return (win[0].indirect(off[0]), win, off)

    def need(q, outs, ins):
        want = {}
        for kind, lst in (("w", outs), ("r", ins)):
            for _, name, lo, hi in lst:
                bank = name in PSUM
                for k2, l2, h2, q2, sem, val in hist.get(name, ()):
                    if q2 == q and q != "dma" and (k2 == "r" or q == "p" and kind == "w"):
                        continue
                    if not (bank and q2 != q) and (k2 == kind == "r" or h2 <= lo or l2 >= hi):
                        continue
                    want[sem] = max(want.get(sem, 0), val)
        return want

    def waits(q, want):
        for sem, val in sorted(want.items()):
            if seen[q].get(sem, 0) < val:
                Q[q].wait_ge(T.sem[sem], val)
                seen[q][sem] = val
                for s2, v2 in snap.get((sem, val), {}).items():
                    seen[q][s2] = max(seen[q].get(s2, 0), v2)

    def note(q, sem, val, outs, ins, known):
        snap[(sem, val)] = dict(known)
        for kind, lst in (("w", outs), ("r", ins)):
            for _, name, lo, hi in lst:
                h = hist.setdefault(name, [])
                if kind == "w":
                    h[:] = [e for e in h if not (e[1] >= lo and e[2] <= hi)]
                h.append((kind, lo, hi, q, sem, val))

    def flat(lst):
        r = []
        for x in lst:
            r += [x] if isinstance(x[1], str) else [x[1], x[2]]
        return r

    def do(q, fn, outs, ins):
        o, i = flat(outs), flat(ins)
        waits(q, need(q, o, i))
        cnt[q] += 1
        fn().then_inc(T.sem[q], 1)
        note(q, q, cnt[q], o, i, seen[q])

    def dma(q, sem, out, in_, outs, ins):
        waits(q, need("dma", outs, ins))
        Q[q].dma_start(out, in_).then_inc(T.sem[sem], 16)
        note("dma", sem, 16, outs, ins, seen[q])

    V, S, P = g.vector, g.scalar, g.tensor

    def copy(out, in_):
        do("v", lambda: V.tensor_copy(out[0], in_[0]), [out], [in_])

    def tt(out, x, y, op):
        if isinstance(out[1], tuple):
            do("v", lambda: V.tensor_tensor(out[0], x[0], y[0], op), [out[1]], [x, y, out[2]])
        else:
            do("v", lambda: V.tensor_tensor(out[0], x[0], y[0], op), [out], [x, y])

    def ts(out, x, s1, op0, s2=None, op1=None):
        ins = [x] + [s for s in (s1, s2) if isinstance(s, tuple)]
        c = [s[0] if isinstance(s, tuple) else s for s in (s1, s2)]
        if op1 is None:
            do("v", lambda: V.tensor_scalar(out[0], x[0], c[0], None, op0), [out], ins)
        else:
            do("v", lambda: V.tensor_scalar(out[0], x[0], c[0], c[1], op0, op1), [out], ins)

    def scan(out, d0, d1, op0, op1):
        do("v", lambda: V.tensor_tensor_scan(out[0], d0[0], d1[0], 1000000.0, op0, op1), [out], [d0, d1])

    def fill(out, val):
        do("v", lambda: V.memset(out[0], val), [out], [])

    def act(out, in_, func, **kw):
        do("s", lambda: S.activation(out[0], in_[0], func, **kw), [out], [in_])

    def mm(out, l, r, start, stop):
        do("p", lambda: P.matmul(out[0], l[0], r[0], start, stop), [out], [l, r])

    def iota(out, pattern, base, cm, **kw):
        do("g", lambda: g.iota(out[0], pattern, base, cm, **kw), [out], [])

    def asel(out, in_, pattern, cop, base, cm):
        do("g", lambda: g.affine_select(out[0], in_[0], pattern, cop, 0.0, base, cm), [out], [in_])

    dma("y", "lp", T.np_[:], T.ph[:], [a("np_")], [])
    dma("s", "lk", T.nk[:], T.ka[:], [a("nk")], [])
    dma("y", "lx", T.xt0[:, 0:2048], T.x0[:], [a("xt0", 0, 2048)], [])

    small = dict(allow_small_or_imprecise_dtypes=True)
    iota(a("pi"), [[0, 2]], 0, 1)
    fill(a("ones"), 1.0)
    asel(a("gm"), a("ones"), [[-16, 8], [0, 16]], Op.is_ge, 0, 1)
    asel(a("gm"), a("gm"), [[16, 8], [0, 16]], Op.is_ge, 15, -1)
    asel(a("idn"), a("ones"), [[1, 128]], Op.is_equal, 0, -1)
    iota(a("cj"), [[0, 16], [4, 16]], 1, 0, **small)
    iota(a("lk"), [[0, 4], [1, 16], [0, 4]], 0, 0)
    iota(a("lz"), [[1, 4], [0, 64]], 1, 0)
    iota(a("ls"), [[0, 64], [2, 2], [0, 2]], -1, 0)
    iota(a("q16"), [[16, 16]], 0, 0, **small)
    asel(a("tri"), a("gm"), [[1, 128]], Op.is_gt, 0, -1)
    iota(a("i1"), [[1, 16], [0, 8], [1, 16]], -1, 0)
    iota(a("i2"), [[256, 16], [1, 128]], 0, 0)
    fill(a("z1"), 0.0)
    fill(a("zf"), 0.0)
    fill(a("xt0", 2048, 2304), 0.0)
    fill(a("xt1", 2048, 2304), 0.0)
    ts(a("li"), a("pi"), 15, Op.bitwise_and)
    copy(a("lf"), a("li"))
    copy(a("z1", 15, 143, 16), a("gm", 0, 128, 16))
    ts(a("z64"), a("z1"), 64.0, Op.mult)
    fill(a("rst"), 0.0)
    fill(a("rst", 0, 256, 16), 1000000.0)
    fill(a("thr"), 65536.0)
    fill(a("aa"), 0)
    fill(a("wt0", 0, 2048), 0.0)
    copy(a("p16_0"), a("np_"))
    for h in range(2):
        copy(a("k16_0_%d" % h), a("nk", 128 * h, 128 * h + 128))
    ts(a("kp"), a("nk"), 32.0, Op.add)
    tt(a("l3"), a("lz"), a("ls"), Op.mult)
    tt(a("lz"), a("l3"), a("lk"), Op.add)
    ts(a("l3"), a("lz"), 15, Op.bitwise_and)
    ts(a("lutf"), a("l3"), a("lf", 0, 1), Op.is_equal)
    ts(a("lutk"), a("lk"), a("lf", 0, 1), Op.is_equal)
    copy(a("p32"), a("np_"))
    waits("y", need("dma", [], [a("zf")]))
    g.sync.dma_start(T.kd[:, 0, :], T.zf[0:8, 0:128]).then_inc(T.sem["kz"], 16)
    g.sync.wait_ge(T.sem["kz"], 16)

    def consts1():
        ts(a("st"), a("i1"), 15.0, Op.min, a("lf", 0, 1), Op.is_equal)
        fill(a("st", 0, 2048, 16), 0.0)
        asel(a("st"), a("st"), [[0, 16], [-16, 8], [0, 16]], Op.is_ge, 0, 1)
        asel(a("st"), a("st"), [[0, 16], [16, 8], [0, 16]], Op.is_ge, 15, -1)

    def consts2():
        fill(a("lutm"), 32.0)
        fill(a("lutm", 2, 3), 4096.0)
        fill(a("luto"), 4096.0)
        fill(a("luto", 1, 2), 0.0)
        fill(a("lutp"), 0.0)
        ts(a("lutp", 1, 2), a("lf", 0, 1), 0.0, Op.is_equal)
        fill(a("rs2"), -128.0)
        fill(a("rs2", 0, 256, 16), 1000000.0)
        copy(a("pf"), a("pi"))
        ts(a("pl", 0, 1), a("lf", 0, 1), 256.0, Op.mult, a("pf", 0, 1), Op.add)
        ts(a("cf"), a("q16"), a("lf", 0, 1), Op.add)
        ts(a("c16"), a("cf"), 16.0, Op.mult)
        ts(a("cd"), a("cf"), 2048.0, Op.add)
        ts(a("cw", 0, 8), a("cf", 0, 8), 3968.0, Op.add)
        ts(a("cw", 8, 16), a("cf", 8, 16), 3840.0, Op.add)
        ts(a("dg_"), a("i2"), a("pl", 0, 1), Op.is_equal)

    def lanes(out, z, src, c, first):
        for i in range(16):
            mm(out, a(z, 15 - i, 143 - i), a3(src, 4 * c, 4 * c + 4, 16 * i, 16 * i + 16), first and i == 0, i == 15)

    dmas = {"kd": 0, "wd": 0}

    def next_table(t):
        x, n = "xt%d" % (t % 2), "xt%d" % ((t + 1) % 2)
        dma("y", "xc%d" % t, T[n][:, 0:2048], T[x][:, 0:2048], [a(n, 0, 2048)], [a(x, 0, 2048)])

    def shifted1(k):
        z = ("bT", "bZ")[k % 2]
        for u in range(4 * k, min(4 * k + 4, 18)):
            o, s = 128 * (u - 4 * k), 0 if u == 16 else 128 * min(u + 1, 15)
            mm(a(z, o, o + 128), a("idn") if u == 17 else a("st", s, s + 128), a("kh"), True, True)
        if k < 4:
            act(a("wt1", 512 * k, 512 * k + 512), a(z), AF.Copy)
        else:
            act(a("wt1", 2048, 2176), a(z, 0, 128), AF.Copy)
            act(a("wt1", 3968, 4096), a(z, 128, 256), AF.Copy)

    def shifted0():
        y, w, k = g.sync, "wd", "kd"

        def start(sem, out, in_):
            y.dma_start(out, in_).then_inc(T.sem[sem], 16)
            dmas[sem] += 16

        if dmas[w]:
            waits("y", {w: dmas[w]})
        kp = a("kp", 0, 128)
        waits("y", need("dma", [], [kp]))
        start(k, T.kd[:, 1:17, :], kp[0])
        for r in range(15):
            start(k, T.kd[:, 17 + r, :], T.kp[15:128:16, 0:128])
        note("dma", k, dmas[k], [], [kp], {})
        waits("y", need("dma", [a("wt0")], []))
        start(w, T.wt0[:, 3968:4096], kp[0])
        y.wait_ge(T.sem[k], dmas[k])
        for j in range(1, 16):
            start(w, T.wt0[j:128:16, 0:2048], T.kd[:, 1 + j:17 + j, :])
        start(w, T.wt0[:, 2048:2176], T.kd[:, 0:16, :])
        note("dma", w, dmas[w], [a("wt0")], [kp], {})

    sent = [0]
    nxt, prv = T.cores[(rank + 1) % n_ranks], T.cores[(rank - 1) % n_ranks]
    n_k = len(topo.engines(prv, core))
    n_p = len(topo.engines(nxt, core))

    def send(name, dst_name, dst, sem, n_in):
        rid, pid = topo.addr(dst, core)
        waits("g", need("g", [], [a(name)]))
        g.remote_dma(T[dst_name][:], T[name][:], T.sem[sem], T.sem["sent"], pid, rid, topo.mask(core, dst))
        sent[0] += len(topo.engines(core, dst))
        note("dma", sem, n_in, [a(dst_name)], [], {})

    def gather_y(t, c):
        act(a("yg", 1024 * c, 1024 * c + 1024), ind(a("xt%d" % (t % 2)), a("p16_%d" % t, 64 * c, 64 * c + 64)), AF.Copy)

    for t in range(RO):
        last, first = t == RO - 1, t == 0
        xt, xn = "xt%d" % (t % 2), "xt%d" % ((t + 1) % 2)

        def d_chunk(t, c):
            for q in range(4 * c, 4 * c + 4):
                tt(row("d3", q), ind(a("xt%d" % (t % 2)), a("k16_%d_%d" % (t, q // 8), 16 * (q % 8), 16 * (q % 8) + 16)),
                   a("yg", 256 * q, 256 * q + 256), Op.subtract)

        def d_abs(c):
            act(a3("a3", 4 * c, 4 * c + 4), a3("d3", 4 * c, 4 * c + 4), AF.Abs)

        def t_sum(c):
            lanes(a(("bT", "bT2")[c // 2], 64 * c, 64 * c + 64), "z1", "d3", c, True)

        def d_sum(c):
            o = a(("bD", "bD2")[c // 2], 64 * c, 64 * c + 64)
            mm(o, a("idn"), a("cj", 64 * c, 64 * c + 64), True, False)
            lanes(o, "z64", "a3", c, False)

        def sign(h):
            s = (128 * h, 128 * h + 128)
            act(a("sn", *s), a(("bT", "bT2")[h], *s), AF.Sign)

        def s_gather(c):
            lo = 64 * (c % 2)
            act(a("sg", 1024 * c, 1024 * c + 1024), ind(a(xt), a("k16_%d_%d" % (t, c // 2), lo, lo + 64)), AF.Copy)

        def least(h):
            s, m = (128 * h, 128 * h + 128), (8 * h, 8 * h + 8)
            tt(a("code", *s), a(("bD", "bD2")[h], *s), a("sn", *s), Op.add)
            scan(a("mi", *s), a("rst", *s), a("code", *s), Op.max, Op.min)
            ts(a("v8", *m), a("mi", s[0] + 15, s[1], 16), 255, Op.bitwise_and)
            copy(a("l8", *m), a("v8", *m))
            tt(a("nsel", *s), ind(a("lutf"), a("l8", *m)), a("p32", *s), Op.mult)
            mm(a("bN", *s), a("gm"), a("nsel", *s), True, True)

        def heads(h):
            copy(a("nb", 128 * h, 128 * h + 128), a("bN", 128 * h, 128 * h + 128))

        def plus(t, h):
            ts(a("kp", 128 * h, 128 * h + 128), a("k16_%d_%d" % (t, h)), 32.0, Op.add)

        def half1():
            copy(a("kh"), a("k16_%d_1" % t))

        def near(c):
            s = (1024 * c, 1024 * c + 1024)
            tt(a("eg", *s), ind(a(xt), a("nb", 64 * c, 64 * c + 64)), a("sg", *s), Op.subtract)

        def near_abs(c):
            act(a3("ae", 4 * c, 4 * c + 4), a("eg", 1024 * c, 1024 * c + 1024), AF.Abs)

        def near_sum(c):
            lanes(a(("bD", "bD2")[c // 2], 64 * c, 64 * c + 64), "z1", "ae", c, True)

        def arrays(h):
            s, m = (128 * h, 128 * h + 128), (8 * h, 8 * h + 8)
            ts(a("ew", *s), a(("bD", "bD2")[h], *s), 1040.0, Op.is_lt, -2048.0, Op.mult)
            scan(a("ms", *s), a("rs2", *s), a("ew", *s), Op.add, Op.min)
            tt(a("o1", *m), a("ms", s[0] + 15, s[1], 16), a("npx", *m), Op.max)
            tt(a("o2", *m), a("o1", *m), a("cw", *m), Op.add)
            copy(a("o16", *m), a("o2", *m))
            tt(a("fr", *s), ind(a("wt%d" % h), a("o16", *m)), a("nfix", *s), Op.add)
            out = a("yk32", *s) if last else a("ks_%d_%d" % (t, h))
            if h == 0:
                ts(out, a("fr", *s), -32.0, Op.add)
            else:
                copy(out, a("fr", *s))
            if not last:
                send("ks_%d_%d" % (t, h), "k16_%d_%d" % (t + 1, h), nxt, "ka%d_%d" % (t + 1, h), n_k)

        def fates():
            mc = a("mi", 15, 256, 16)
            ts(a("lt"), mc, a("thr"), Op.is_lt)
            ts(a("kf"), mc, 53248.0, Op.is_lt)
            tt(a("ksel"), ind(a("lutk"), a("l8")), a("p32"), Op.mult)
            mm(a("bM", 32, 48), a("gm"), a("kf"), True, True)
            mm(a("bT2", 0, 256), a("gm"), a("ksel"), True, True)
            tt(a("fl"), a("lt"), a("kf"), Op.add)
            copy(a("fl16"), a("fl"))

        def names():
            act(a("pks"), a("bT2", 0, 256), AF.Copy)
            act(a("ns", 0, 128), a("bN", 0, 128), AF.Copy, bias=32.0)
            act(a("ns", 128, 256), a("bN", 128, 256), AF.Copy)

        def phages():
            tt(a("pa"), ind(a("lutm"), a("fl16")), a("kp"), Op.min)
            ts(a("kk"), a("v8"), 2, Op.logical_shift_right, 15, Op.bitwise_and)
            tt(a("pt"), a("pa"), a("p32"), Op.mult)
            tt(a("ok"), a("kk"), a("c16"), Op.add)
            ts(a("pn"), a("pt"), 5, Op.logical_shift_right, 2047, Op.bitwise_and)
            copy(a("ok16"), a("ok"))
            if last:
                copy(a("yp32"), a("pn"))
                dma("y", "op", T.yp[:], T.yp32[:], [], [a("yp32")])
            else:
                copy(a("ps_%d" % t), a("pn"))
                send("ps_%d" % t, "p16_%d" % (t + 1), prv, "pa%d" % (t + 1), n_p)

        def lanes_k():
            act(a("yk_"), ind(a("yg"), a("ok16")), AF.Copy)
            act(a("sgn"), ind(a("yg"), a("ok16")), AF.Sign, scale=-1.0, bias=127.5)

        def writers():
            tt(a("rr"), ind(a("luto"), a("fl16")), a("pks"), Op.max)
            for i in range(16):
                mm(a("bM", 0, 16), a("dg_", 128 * i, 128 * i + 128), a("rr", i, 256, 16), i == 0, i == 15)

        def values():
            tt(a("dk"), ind(a("sg"), a("ok16")), a("yk_"), Op.subtract)
            act(a("adk"), a("dk"), AF.Abs)
            tt(a("nfix"), ind(a("lutp"), a("fl16")), a("ns"), Op.mult)
            ts(a("npx"), a("fl"), 1.0, Op.is_equal, -8192.0, Op.mult)

        def equals():
            copy(a("ol"), a("bM", 0, 16))
            for q in range(16):
                ts(a("eq", 272 * q, 256 * q + 256), a("rr", 16 * q, 256), a("ol", q, q + 1), Op.is_equal)
                mm(a("bC", 16 * q, 16 * q + 16), a("tri"), a("eq", 272 * q, 272 * q + 16), q == 0, q in (0, 15))
                if q < 15:
                    mm(a("bC", 16 * q + 16, 256), a("gm"), a("eq", 272 * q + 16, 256 * q + 256), q == 0, False)

        def counts():
            act(a("cs"), a("bC", 0, 256), AF.Copy, scale=4096.0)
            for i in range(16):
                mm(a("bM", 16, 32), a("dg_", 128 * i, 128 * i + 128), a("cs", i, 256, 16), i == 0, i == 15)

        def change():
            ts(a("c1"), a("adk"), 32.0, Op.is_le, 128.0, Op.mult)
            tt(a("tt"), a("c1"), a("sgn"), Op.mult)

        def scatter():
            tt(a("v1"), a("bM", 16, 32), a("ol"), Op.add)
            tt(a("v2"), a("v1"), a("cd"), Op.min)
            copy(a("w16"), a("v2"))
            tt(ind(a(xn), a("w16")), a("yk_"), a("tt"), Op.add)

        def allowance():
            do("v", lambda: V.tensor_reduce(T.ca[:], T.bM[:, 32:48], AX.X, Op.add), [a("ca")], [a("bM", 32, 48)])
            tt(a("aa"), a("aa"), a("ca"), Op.add)
            ts(a("ab"), a("aa"), 15, Op.bitwise_and)
            ts(a("thr"), a("ab"), 256.0, Op.mult, 65536.0, Op.add)

        next_table(t)
        if first:
            shifted0()
            for c in range(4):
                gather_y(0, c)
            d_chunk(0, 0)
            d_chunk(0, 1)
        steps = {"le0": lambda: (consts1() if first else None, least(0)), "le1": lambda: least(1),
                 "he0": lambda: (consts2() if first else None, heads(0)), "he1": lambda: heads(1),
                 "dc2": lambda: d_chunk(t, 2), "dc3": lambda: d_chunk(t, 3), "sn0": lambda: sign(0), "sn1": lambda: sign(1),
                 "fa": fates, "pk": names, "kh": half1, "wr": writers, "ph": phages, "yk": lanes_k, "eq": equals, "va": values,
                 "co": counts, "ch": change, "sc": scatter, "ar0": lambda: arrays(0), "ar1": lambda: arrays(1)}
        for c in range(4):
            for x, f in (("ts", t_sum), ("da", d_abs), ("ds", d_sum), ("sg", s_gather), ("n", near), ("na", near_abs), ("nl", near_sum)):
                steps["%s%d" % (x, c)] = lambda f=f, c=c: f(c)
        for k in range(5):
            steps["sh%d" % k] = lambda k=k: shifted1(k)
        if not first:
            steps["pl1"] = lambda: plus(t, 1)
        if not last:
            steps.update({"al": allowance, "p32": lambda: copy(a("p32"), a("p16_%d" % (t + 1))), "pl0": lambda: plus(t + 1, 0),
                          "w0": shifted0, "dc0": lambda: d_chunk(t + 1, 0), "dc1": lambda: d_chunk(t + 1, 1)})
            for c in range(4):
                steps["y%d" % c] = lambda c=c: gather_y(t + 1, c)
        for x in ORDER.split():
            if x in steps:
                steps[x]()
            if x == "sc" and last:
                dma("y", "oy", T.yx[:], T[xn][:, 0:2048], [], [a(xn, 0, 2048)])
        if last:
            dma("y", "ok", T.yk[:], T.yk32[:], [], [a("yk32")])
    g.wait_ge(T.sem["sent"], sent[0])
    for s in ("oy", "ok", "op"):
        g.sync.wait_ge(T.sem[s], 16)
    for q in cnt:
        if seen["y"].get(q, 0) < cnt[q]:
            g.sync.wait_ge(T.sem[q], cnt[q])
